import numpy as np, ml_dtypes
CORES = [36,38,116,118,124,126,164,166,244,246,252,254]
N = 12
import mx_ref
NC, K, S = 128, 2, 2
CNT = [[0,8,12,24,20,20,12,12,8,12,0,0],[8,0,0,8,44,24,4,0,12,0,28,0],[0,0,0,60,0,28,8,24,0,8,0,0],[52,0,0,0,20,4,8,0,12,4,8,20],[4,16,0,0,0,0,0,8,4,20,32,44],[4,8,24,0,4,0,0,8,16,20,12,32],[16,32,20,0,0,0,0,8,24,20,0,8],[8,12,4,12,0,0,12,0,28,24,20,8],[8,0,16,16,32,8,0,4,0,16,28,0],[16,40,32,8,0,0,20,0,8,0,0,4],[12,12,20,0,0,28,32,8,0,4,0,12],[0,0,0,0,8,16,32,56,16,0,0,0]]
OFF = [[sum(c[:f]) for f in range(N + 1)] for c in CNT]
BF = ml_dtypes.bfloat16
def setup_inputs(rng):
    def f(*shape):
        return mx_ref.flush((rng.standard_normal(shape, dtype=np.float32) * np.exp2(rng.integers(-2, 3, shape[:-1] + (1,)))).astype(BF))
    return {"w": f(N, 128, 512), "x": f(N, 128, 4 * NC)}
def setup_inputs_blocks(rng):
    d = setup_inputs(rng)
    for k in ("w", "x"): d[k] = mx_ref.spread(d[k], rng, 1)
    return d
def setup_inputs_wide(rng):
    d = setup_inputs(rng)
    for k in ("x",): d[k] = mx_ref.flush((d[k].astype(np.float32) * np.exp2(rng.integers(-8, 9, (N, 1, 1))).astype(np.float32)).astype(BF))
    return d
def setup_inputs_zeros(rng):
    d = setup_inputs(rng); v = d["x"].reshape(N, 128, -1, 4).copy()
    v[np.broadcast_to((rng.random((N, 1, v.shape[2], 1)) < 0.33), v.shape)] = 0
    d["x"] = v.reshape(d["x"].shape)
    return d
def reference(w, x):
    y = np.zeros((N, 128, NC), np.float32)
    for k in range(K):
        for e in range(N):
            f = (e - S * k) % N
            t = np.concatenate([x[j][:, 4 * OFF[j][f]:4 * OFF[j][f + 1]] for j in range(N)], axis=1)
            p = mx_ref.matmul(mx_ref.quantize(w[e]), mx_ref.quantize(t)); c = 0
            for j in range(N):
                a, b = OFF[j][f], OFF[j][f + 1]
                y[j][:, a:b] = p[:, c:c + b - a] if k == 0 else y[j][:, a:b] + p[:, c:c + b - a]; c += b - a
    return {"y": y}

@@ -1,0 +1,281 @@
+from concourse.bass import DstId, RemoteDMATransfer
+from concourse.mybir import dt
+
+P = 128
+STEP = 2
+CLS = (16, 32, 64)
+TW = 512
+XB = TW - P
+NH = 2
+ROW = 40.0
+BYTE = 0.07
+LATE1 = 7000.0
+COLD = 2500.0
+SITE = 1500.0
+
+SCRATCH = {
+    "xb": ("sbuf", [P, 512], "bfloat16"),
+    "wb": ("sbuf", [P, 512], "bfloat16"),
+    "wq": ("sbuf", [P, P], "float8_e4m3fn_x4"),
+    "ws": ("sbuf", [P, P], "uint8"),
+    "vq": ("sbuf", [P, P], "float8_e4m3fn_x4"),
+    "vs": ("sbuf", [P, P], "uint8"),
+    "tq": ("sbuf", [P, TW], "float8_e4m3fn_x4"),
+    "ts": ("sbuf", [P, TW], "uint8"),
+    "ps": ("psum", [P, 512], "float32"),
+    "rs": ("sbuf", [P, XB], "float32"),
+    "yl": ("sbuf", [P, P], "float32"),
+}
+SEMAPHORES = ["lx", "lw", "qx", "qw", "hx", "hw", "w2", "tok", "mm", "cp", "res", "st", "loc"]
+
+CACHE = {}
+
+
+def engines_of(mask):
+    return [e for e in range(mask.bit_length()) if (mask >> e) & 1]
+
+
+def split(k, avail):
+    counts = [1] * k
+    grown = True
+    while grown:
+        grown = False
+        for i in range(k):
+            if counts[i] == min(counts) and sum(counts) + counts[i] <= avail:
+                counts[i] *= 2
+                grown = True
+    return counts
+
+
+def make_calls(core, trs, topo, load):
+    groups = {}
+    for t in trs:
+        groups.setdefault((t["prio"], -t["nb"]), []).append(t)
+    calls = []
+    for key in sorted(groups):
+        todo = groups[key]
+        nb = -key[1]
+        while todo:
+            fars, nears, rest = [], [], []
+            for t in todo:
+                allowed = len(engines_of(topo.mask(core, t["dst"])))
+                if len(fars) + len(nears) >= len(load):
+                    rest.append(t)
+                elif allowed == len(load):
+                    nears.append(t)
+                elif len(fars) < allowed:
+                    fars.append(t)
+                else:
+                    rest.append(t)
+            todo = rest
+            free = set(load)
+            for part in (fars, nears):
+                if not part:
+                    continue
+                allowed = [e for e in engines_of(topo.mask(core, part[0]["dst"])) if e in free]
+                counts = split(len(part), len(allowed))
+                for t, c in sorted(zip(part, counts), key=lambda tc: tc[1]):
+                    pick = sorted([e for e in allowed if e in free], key=lambda e: (load[e], e))[:c]
+                    t["mask"] = sum(1 << e for e in pick)
+                    t["eng"] = c
+                    for e in pick:
+                        free.discard(e)
+                        load[e] += (P // c) * (ROW + BYTE * nb)
+            calls.append(fars + nears)
+    return calls
+
+
+def build_plan(cores, cnt, topo):
+    n = len(cores)
+    off = [[sum(row[:f]) for f in range(n + 1)] for row in cnt]
+    world = range(2 * max(cores) + 2)
+
+    def on_chip(a, b):
+        return topo.host(a) == topo.host(b) and topo.chip(a) == topo.chip(b)
+
+    def reach(d):
+        return sum(1 for e in cores if topo.may_write(d, e))
+
+    def width(k):
+        return min(w for w in CLS if w >= k)
+
+    far = min(len(engines_of(topo.mask(a, b))) for a in cores for b in cores if a != b and topo.may_write(a, b))
+
+    def cost(nbs):
+        return sum((P / far) * (ROW + BYTE * nb) for nb in nbs)
+
+    aides = {j: [] for j in range(n)}
+    taken = set(cores)
+    for k in range(NH):
+        for j in sorted(range(n), key=lambda i: reach(cores[i])):
+            c = cores[j]
+            pool = [d for d in world if on_chip(c, d) and d not in taken]
+            if pool:
+                best = min(pool, key=lambda d: (-reach(d), topo.die(d) != topo.die(c), d))
+                aides[j].append(best)
+                taken.add(best)
+
+    def schedule(fin, items):
+        who = {}
+        items = sorted(items, key=lambda it: (sum(1 for a in fin if topo.may_write(a, it[1])), -it[2]))
+        for key, dst, wgt in items:
+            a = min((a for a in fin if topo.may_write(a, dst) and a != dst), key=lambda a: (fin[a] + wgt, a))
+            fin[a] += wgt
+            who[key] = a
+        return who
+
+    warm = set(a for j in range(n) for a in aides[j])
+    for turn in range(2):
+        site = {}
+        for f in range(n):
+            fin = {cores[f]: 0.0}
+            for a in aides[f]:
+                fin[a] = SITE + (0.0 if a in warm else COLD)
+            got = schedule(fin, [((j, f), cores[j], cost((4 * cnt[j][f],))) for j in range(n) if cnt[j][f]])
+            site.update(got)
+        sites = {f: sorted(set(site[(j, f)] for j in range(n) if cnt[j][f]) | set([cores[f]])) for f in range(n)}
+        who1 = {}
+        for j in range(n):
+            c = cores[j]
+            fin = {c: 0.0}
+            for a in aides[j]:
+                fin[a] = LATE1
+            items = [(("t", j, f), site[(j, f)], cost((4 * width(cnt[j][f]), width(cnt[j][f])))) for f in range(n) if cnt[j][f]]
+            items += [(("w", j, s), s, cost((4 * P, P))) for s in sites[(j - STEP) % n]]
+            for it in [i for i in items if on_chip(c, i[1])]:
+                who1[it[0]] = c
+            who1.update(schedule(fin, [i for i in items if not on_chip(c, i[1])]))
+        warm = set(who1.values())
+
+    slot, valid, tile = {}, {}, {}
+    for f in range(n):
+        for s in sites[f]:
+            srcs = [j for j in range(n) if cnt[j][f] and site[(j, f)] == s]
+            total = sum(width(cnt[j][f]) for j in srcs)
+            tile[s] = total
+            at = XB - total
+            for j in srcs:
+                w = width(cnt[j][f])
+                lo = min(off[j][f], P - w)
+                slot[(j, f)] = (at, lo, w)
+                valid[(j, f)] = at - (XB - total) + off[j][f] - lo
+                at += w
+
+    def tr(src, dst, kind, sb, slo, shi, db, dlo, sem, need, prio):
+        return {"src": src, "dst": dst, "kind": kind, "sb": sb, "slo": slo, "shi": shi, "db": db, "dlo": dlo,
+                "dhi": dlo + shi - slo, "sem": sem, "need": need, "prio": prio,
+                "nb": (shi - slo) * (1 if kind == "s" else 4)}
+
+    st1, st2 = {}, {}
+    for j in range(n):
+        c = cores[j]
+        mine = st1.setdefault(c, [])
+        for a in aides[j]:
+            if any(who1[k] == a for k in who1 if k[0] == "t" and k[1] == j) or (a in sites[j] and tile[a] < P):
+                mine.append(tr(c, a, "c", "tq", XB, TW, "tq", XB, "hx", "qx", 0))
+                mine.append(tr(c, a, "s", "ts", XB, TW, "ts", XB, "hx", "qx", 0))
+            if any(who1[k] == a for k in who1 if k[0] == "w" and k[1] == j) or a in sites[j]:
+                mine.append(tr(c, a, "c", "wq", 0, P, "wq", 0, "hw", "qw", 1))
+                mine.append(tr(c, a, "s", "ws", 0, P, "ws", 0, "hw", "qw", 1))
+        for s in sites[(j - STEP) % n]:
+            a = who1[("w", j, s)]
+            need = "qw" if a == c else "hw"
+            prio = 1 if a == c else 3
+            st1.setdefault(a, []).append(tr(a, s, "c", "wq", 0, P, "vq", 0, "w2", need, prio))
+            st1.setdefault(a, []).append(tr(a, s, "s", "ws", 0, P, "vs", 0, "w2", need, prio))
+        for f in range(n):
+            if cnt[j][f]:
+                a = who1[("t", j, f)]
+                at, lo, w = slot[(j, f)]
+                need = "qx" if a == c else "hx"
+                st1.setdefault(a, []).append(tr(a, site[(j, f)], "c", "tq", XB + lo, XB + lo + w, "tq", at, "tok", need, 2))
+                st1.setdefault(a, []).append(tr(a, site[(j, f)], "s", "ts", XB + lo, XB + lo + w, "ts", at, "tok", need, 2))
+                v = valid[(j, f)]
+                st2.setdefault(site[(j, f)], []).append(tr(site[(j, f)], c, "f", "rs", v, v + cnt[j][f], "yl", off[j][f],
+                                                           "res", "cp", 4))
+
+    calls, expect = {}, {}
+    for stage in (st1, st2):
+        for c in sorted(stage):
+            full = max(len(engines_of(topo.mask(c, d))) for d in world if on_chip(c, d) and d != c)
+            made = make_calls(c, stage[c], topo, {e: 0.0 for e in range(full)})
+            calls.setdefault(c, []).extend(made)
+            for call in made:
+                for t in call:
+                    expect.setdefault(t["dst"], {}).setdefault(t["sem"], 0)
+                    expect[t["dst"]][t["sem"]] += t["eng"]
+                    expect.setdefault(c, {}).setdefault("loc", 0)
+                    expect[c]["loc"] += t["eng"]
+    return {"calls": calls, "expect": expect, "tile": tile}
+
+
+def view(T, kind, name, lo, hi):
+    v = T[name][:, lo:hi]
+    return v.bitcast(dt.uint8) if kind == "c" else v
+
+
+def rank_program(g, core, T, topo):
+    if "plan" not in CACHE:
+        CACHE["plan"] = build_plan(list(T.cores), T.tables["CNT"], topo)
+    plan = CACHE["plan"]
+    calls = plan["calls"].get(core, [])
+    expect = plan["expect"].get(core, {})
+    rank = T.rank_of(core)
+    if rank is None and not calls:
+        return
+    sem = T.sem
+    count = {"qx": 1, "qw": 1, "cp": 1}
+    count.update(expect)
+
+    if rank is not None:
+        g.sync.dma_start(T.xb[:], T.x[:]).then_inc(sem.lx, 16)
+        g.scalar.dma_start(T.wb[:], T.w[:]).then_inc(sem.lw, 16)
+        g.vector.wait_ge(sem.lx, 16)
+        g.vector.quantize_mx(T.tq[:, XB:TW], T.ts[:, XB:TW], T.xb[:]).then_inc(sem.qx, 1)
+        g.vector.wait_ge(sem.lw, 16)
+        g.vector.quantize_mx(T.wq[:], T.ws[:], T.wb[:]).then_inc(sem.qw, 1)
+
+    if core in plan["tile"]:
+        got = plan["tile"][core]
+        lo = XB - got
+        m = max(got, P)
+        g.tensor.wait_ge(sem.qw if rank is not None else sem.hw, count["qw" if rank is not None else "hw"])
+        if got < P:
+            g.tensor.wait_ge(sem.qx if rank is not None else sem.hx, count["qx" if rank is not None else "hx"])
+        if got:
+            g.tensor.wait_ge(sem.tok, count["tok"])
+        g.tensor.matmul_mx(T.ps[:, 0:m], T.wq[:], T.ws[:], T.tq[:, lo:lo + m], T.ts[:, lo:lo + m], True, False).then_inc(sem.mm, 1)
+        g.tensor.wait_ge(sem.w2, count["w2"])
+        g.tensor.matmul_mx(T.ps[:, 0:m], T.vq[:], T.vs[:], T.tq[:, lo:lo + m], T.ts[:, lo:lo + m], False, True).then_inc(sem.mm, 1)
+        g.vector.wait_ge(sem.mm, 2)
+        if got:
+            g.vector.tensor_copy(T.rs[:, 0:got], T.ps[:, 0:got]).then_inc(sem.cp, 1)
+
+    waited = set()
+    for call in calls:
+        for t in call:
+            if t["need"] not in waited:
+                waited.add(t["need"])
+                g.wait_ge(sem[t["need"]], count[t["need"]])
+        made = []
+        for t in call:
+            rid, pid = topo.addr(t["dst"], core)
+            made.append((view(T, t["kind"], t["sb"], t["slo"], t["shi"]), view(T, t["kind"], t["db"], t["dlo"], t["dhi"]),
+                         rid, pid, t["mask"], sem[t["sem"]]))
+        if len(made) == 1:
+            src, dst, rid, pid, mask, rsem = made[0]
+            g.remote_dma(out_ap=dst, in_ap=src, remote_sem=rsem, local_sem=sem.loc, pid=pid, routing_id=rid,
+                         dma_engine_mask=mask)
+        else:
+            g.remote_dma_fused([RemoteDMATransfer(dst_ids=[DstId(rid=rid, pnc=pid)], dma_engine_mask=mask, remote_sem=rsem,
+                                                  src=src, dst=dst) for src, dst, rid, pid, mask, rsem in made],
+                               local_sem=sem.loc)
+    for name in ("hx", "hw"):
+        if name in expect and name not in waited and not (core in plan["tile"] and (name == "hw" or plan["tile"][core] < P)):
+            g.wait_ge(sem[name], count[name])
+    if rank is not None:
+        g.sync.wait_ge(sem.res, count["res"])
+        g.sync.dma_start(T.y[:], T.yl[:]).then_inc(sem.st, 16)
+        g.sync.wait_ge(sem.st, 16)
+    if calls:
+        g.wait_ge(sem.loc, count["loc"])

@@ -9,7 +9,7 @@ XB = TW - P
 NH = 2
 ROW = 40.0
 BYTE = 0.07
-LATE1 = 7000.0
+LATE1 = 4000.0
 COLD = 2500.0
 SITE = 1500.0
 
@@ -129,19 +129,23 @@ def build_plan(cores, cnt, topo):
         site = {}
         for f in range(n):
             fin = {cores[f]: 0.0}
-            for a in aides[f]:
+            for a in aides[f] if topo.may_write(cores[(f + STEP) % n], cores[f]) else aides[f][:1]:
                 fin[a] = SITE + (0.0 if a in warm else COLD)
-            got = schedule(fin, [((j, f), cores[j], cost((4 * cnt[j][f],))) for j in range(n) if cnt[j][f]])
-            site.update(got)
+            site.update(schedule(fin, [((j, f), cores[j], cost((4 * cnt[j][f],))) for j in range(n) if cnt[j][f]]))
         sites = {f: sorted(set(site[(j, f)] for j in range(n) if cnt[j][f]) | set([cores[f]])) for f in range(n)}
         who1 = {}
         for j in range(n):
             c = cores[j]
+            e = (j - STEP) % n
             fin = {c: 0.0}
             for a in aides[j]:
                 fin[a] = LATE1
             items = [(("t", j, f), site[(j, f)], cost((4 * width(cnt[j][f]), width(cnt[j][f])))) for f in range(n) if cnt[j][f]]
-            items += [(("w", j, s), s, cost((4 * P, P))) for s in sites[(j - STEP) % n]]
+            if topo.may_write(c, cores[e]):
+                who1[("w", j, cores[e])] = c
+                fin[c] += cost((4 * P, P))
+            else:
+                items += [(("w", j, s), s, cost((4 * P, P))) for s in sites[e]]
             for it in [i for i in items if on_chip(c, i[1])]:
                 who1[it[0]] = c
             who1.update(schedule(fin, [i for i in items if not on_chip(c, i[1])]))
@@ -169,6 +173,7 @@ def build_plan(cores, cnt, topo):
     st1, st2 = {}, {}
     for j in range(n):
         c = cores[j]
+        e = (j - STEP) % n
         mine = st1.setdefault(c, [])
         for a in aides[j]:
             if any(who1[k] == a for k in who1 if k[0] == "t" and k[1] == j) or (a in sites[j] and tile[a] < P):
@@ -177,12 +182,16 @@ def build_plan(cores, cnt, topo):
             if any(who1[k] == a for k in who1 if k[0] == "w" and k[1] == j) or a in sites[j]:
                 mine.append(tr(c, a, "c", "wq", 0, P, "wq", 0, "hw", "qw", 1))
                 mine.append(tr(c, a, "s", "ws", 0, P, "ws", 0, "hw", "qw", 1))
-        for s in sites[(j - STEP) % n]:
-            a = who1[("w", j, s)]
-            need = "qw" if a == c else "hw"
-            prio = 1 if a == c else 3
-            st1.setdefault(a, []).append(tr(a, s, "c", "wq", 0, P, "vq", 0, "w2", need, prio))
-            st1.setdefault(a, []).append(tr(a, s, "s", "ws", 0, P, "vs", 0, "w2", need, prio))
+        for s in sites[e]:
+            if ("w", j, s) in who1:
+                a = who1[("w", j, s)]
+                need = "qw" if a == c else "hw"
+                prio = 1 if a == c else 3
+                st1.setdefault(a, []).append(tr(a, s, "c", "wq", 0, P, "vq", 0, "w2", need, prio))
+                st1.setdefault(a, []).append(tr(a, s, "s", "ws", 0, P, "vs", 0, "w2", need, prio))
+            else:
+                st1.setdefault(cores[e], []).append(tr(cores[e], s, "c", "vq", 0, P, "vq", 0, "w2", "w2", 3))
+                st1.setdefault(cores[e], []).append(tr(cores[e], s, "s", "vs", 0, P, "vs", 0, "w2", "w2", 3))
         for f in range(n):
             if cnt[j][f]:
                 a = who1[("t", j, f)]

from concourse.bass import DstId, RemoteDMATransfer
from concourse.mybir import dt

P = 128
STEP = 2
CLS = (16, 32, 64)
TW = 512
XB = TW - P
NH = 2
ROW = 40.0
BYTE = 0.07
LATE1 = 4000.0
COLD = 2500.0
SITE = 1500.0

SCRATCH = {
    "xb": ("sbuf", [P, 512], "bfloat16"),
    "wb": ("sbuf", [P, 512], "bfloat16"),
    "wq": ("sbuf", [P, P], "float8_e4m3fn_x4"),
    "ws": ("sbuf", [P, P], "uint8"),
    "vq": ("sbuf", [P, P], "float8_e4m3fn_x4"),
    "vs": ("sbuf", [P, P], "uint8"),
    "tq": ("sbuf", [P, TW], "float8_e4m3fn_x4"),
    "ts": ("sbuf", [P, TW], "uint8"),
    "ps": ("psum", [P, 512], "float32"),
    "rs": ("sbuf", [P, XB], "float32"),
    "yl": ("sbuf", [P, P], "float32"),
}
SEMAPHORES = ["lx", "lw", "qx", "qw", "hx", "hw", "w2", "tok", "mm", "cp", "res", "st", "loc"]

CACHE = {}


def engines_of(mask):
    return [e for e in range(mask.bit_length()) if (mask >> e) & 1]


def split(k, avail):
    counts = [1] * k
    grown = True
    while grown:
        grown = False
        for i in range(k):
            if counts[i] == min(counts) and sum(counts) + counts[i] <= avail:
                counts[i] *= 2
                grown = True
    return counts


def make_calls(core, trs, topo, load):
    groups = {}
    for t in trs:
        groups.setdefault((t["prio"], -t["nb"]), []).append(t)
    calls = []
    for key in sorted(groups):
        todo = groups[key]
        nb = -key[1]
        while todo:
            fars, nears, rest = [], [], []
            for t in todo:
                allowed = len(engines_of(topo.mask(core, t["dst"])))
                if len(fars) + len(nears) >= len(load):
                    rest.append(t)
                elif allowed == len(load):
                    nears.append(t)
                elif len(fars) < allowed:
                    fars.append(t)
                else:
                    rest.append(t)
            todo = rest
            free = set(load)
            for part in (fars, nears):
                if not part:
                    continue
                allowed = [e for e in engines_of(topo.mask(core, part[0]["dst"])) if e in free]
                counts = split(len(part), len(allowed))
                for t, c in sorted(zip(part, counts), key=lambda tc: tc[1]):
                    pick = sorted([e for e in allowed if e in free], key=lambda e: (load[e], e))[:c]
                    t["mask"] = sum(1 << e for e in pick)
                    t["eng"] = c
                    for e in pick:
                        free.discard(e)
                        load[e] += (P // c) * (ROW + BYTE * nb)
            calls.append(fars + nears)
    return calls


def build_plan(cores, cnt, topo):
    n = len(cores)
    off = [[sum(row[:f]) for f in range(n + 1)] for row in cnt]
    world = range(2 * max(cores) + 2)

    def on_chip(a, b):
        return topo.host(a) == topo.host(b) and topo.chip(a) == topo.chip(b)

    def reach(d):
        return sum(1 for e in cores if topo.may_write(d, e))

    def width(k):
        return min(w for w in CLS if w >= k)

    far = min(len(engines_of(topo.mask(a, b))) for a in cores for b in cores if a != b and topo.may_write(a, b))

    def cost(nbs):
        return sum((P / far) * (ROW + BYTE * nb) for nb in nbs)

    aides = {j: [] for j in range(n)}
    taken = set(cores)
    for k in range(NH):
        for j in sorted(range(n), key=lambda i: reach(cores[i])):
            c = cores[j]
            pool = [d for d in world if on_chip(c, d) and d not in taken]
            if pool:
                best = min(pool, key=lambda d: (-reach(d), topo.die(d) != topo.die(c), d))
                aides[j].append(best)
                taken.add(best)

    def schedule(fin, items):
        who = {}
        items = sorted(items, key=lambda it: (sum(1 for a in fin if topo.may_write(a, it[1])), -it[2]))
        for key, dst, wgt in items:
            a = min((a for a in fin if topo.may_write(a, dst) and a != dst), key=lambda a: (fin[a] + wgt, a))
            fin[a] += wgt
            who[key] = a
        return who

    warm = set(a for j in range(n) for a in aides[j])
    for turn in range(2):
        site = {}
        for f in range(n):
            fin = {cores[f]: 0.0}
            for a in aides[f] if topo.may_write(cores[(f + STEP) % n], cores[f]) else aides[f][:1]:
                fin[a] = SITE + (0.0 if a in warm else COLD)
            site.update(schedule(fin, [((j, f), cores[j], cost((4 * cnt[j][f],))) for j in range(n) if cnt[j][f]]))
        sites = {f: sorted(set(site[(j, f)] for j in range(n) if cnt[j][f]) | set([cores[f]])) for f in range(n)}
        who1 = {}
        for j in range(n):
            c = cores[j]
            e = (j - STEP) % n
            fin = {c: 0.0}
            for a in aides[j]:
                fin[a] = LATE1
            items = [(("t", j, f), site[(j, f)], cost((4 * width(cnt[j][f]), width(cnt[j][f])))) for f in range(n) if cnt[j][f]]
            if topo.may_write(c, cores[e]):
                who1[("w", j, cores[e])] = c
                fin[c] += cost((4 * P, P))
            else:
                items += [(("w", j, s), s, cost((4 * P, P))) for s in sites[e]]
            for it in [i for i in items if on_chip(c, i[1])]:
                who1[it[0]] = c
            who1.update(schedule(fin, [i for i in items if not on_chip(c, i[1])]))
        warm = set(who1.values())

    slot, valid, tile = {}, {}, {}
    for f in range(n):
        for s in sites[f]:
            srcs = [j for j in range(n) if cnt[j][f] and site[(j, f)] == s]
            total = sum(width(cnt[j][f]) for j in srcs)
            tile[s] = total
            at = XB - total
            for j in srcs:
                w = width(cnt[j][f])
                lo = min(off[j][f], P - w)
                slot[(j, f)] = (at, lo, w)
                valid[(j, f)] = at - (XB - total) + off[j][f] - lo
                at += w

    def tr(src, dst, kind, sb, slo, shi, db, dlo, sem, need, prio):
        return {"src": src, "dst": dst, "kind": kind, "sb": sb, "slo": slo, "shi": shi, "db": db, "dlo": dlo,
                "dhi": dlo + shi - slo, "sem": sem, "need": need, "prio": prio,
                "nb": (shi - slo) * (1 if kind == "s" else 4)}

    st1, st2 = {}, {}
    for j in range(n):
        c = cores[j]
        e = (j - STEP) % n
        mine = st1.setdefault(c, [])
        for a in aides[j]:
            if any(who1[k] == a for k in who1 if k[0] == "t" and k[1] == j) or (a in sites[j] and tile[a] < P):
                mine.append(tr(c, a, "c", "tq", XB, TW, "tq", XB, "hx", "qx", 0))
                mine.append(tr(c, a, "s", "ts", XB, TW, "ts", XB, "hx", "qx", 0))
            if any(who1[k] == a for k in who1 if k[0] == "w" and k[1] == j) or a in sites[j]:
                mine.append(tr(c, a, "c", "wq", 0, P, "wq", 0, "hw", "qw", 1))
                mine.append(tr(c, a, "s", "ws", 0, P, "ws", 0, "hw", "qw", 1))
        for s in sites[e]:
            if ("w", j, s) in who1:
                a = who1[("w", j, s)]
                need = "qw" if a == c else "hw"
                prio = 1 if a == c else 3
                st1.setdefault(a, []).append(tr(a, s, "c", "wq", 0, P, "vq", 0, "w2", need, prio))
                st1.setdefault(a, []).append(tr(a, s, "s", "ws", 0, P, "vs", 0, "w2", need, prio))
            else:
                st1.setdefault(cores[e], []).append(tr(cores[e], s, "c", "vq", 0, P, "vq", 0, "w2", "w2", 3))
                st1.setdefault(cores[e], []).append(tr(cores[e], s, "s", "vs", 0, P, "vs", 0, "w2", "w2", 3))
        for f in range(n):
            if cnt[j][f]:
                a = who1[("t", j, f)]
                at, lo, w = slot[(j, f)]
                need = "qx" if a == c else "hx"
                st1.setdefault(a, []).append(tr(a, site[(j, f)], "c", "tq", XB + lo, XB + lo + w, "tq", at, "tok", need, 2))
                st1.setdefault(a, []).append(tr(a, site[(j, f)], "s", "ts", XB + lo, XB + lo + w, "ts", at, "tok", need, 2))
                v = valid[(j, f)]
                st2.setdefault(site[(j, f)], []).append(tr(site[(j, f)], c, "f", "rs", v, v + cnt[j][f], "yl", off[j][f],
                                                           "res", "cp", 4))

    calls, expect = {}, {}
    for stage in (st1, st2):
        for c in sorted(stage):
            full = max(len(engines_of(topo.mask(c, d))) for d in world if on_chip(c, d) and d != c)
            made = make_calls(c, stage[c], topo, {e: 0.0 for e in range(full)})
            calls.setdefault(c, []).extend(made)
            for call in made:
                for t in call:
                    expect.setdefault(t["dst"], {}).setdefault(t["sem"], 0)
                    expect[t["dst"]][t["sem"]] += t["eng"]
                    expect.setdefault(c, {}).setdefault("loc", 0)
                    expect[c]["loc"] += t["eng"]
    return {"calls": calls, "expect": expect, "tile": tile}


def view(T, kind, name, lo, hi):
    v = T[name][:, lo:hi]
    return v.bitcast(dt.uint8) if kind == "c" else v


def rank_program(g, core, T, topo):
    if "plan" not in CACHE:
        CACHE["plan"] = build_plan(list(T.cores), T.tables["CNT"], topo)
    plan = CACHE["plan"]
    calls = plan["calls"].get(core, [])
    expect = plan["expect"].get(core, {})
    rank = T.rank_of(core)
    if rank is None and not calls:
        return
    sem = T.sem
    count = {"qx": 1, "qw": 1, "cp": 1}
    count.update(expect)

    if rank is not None:
        g.sync.dma_start(T.xb[:], T.x[:]).then_inc(sem.lx, 16)
        g.scalar.dma_start(T.wb[:], T.w[:]).then_inc(sem.lw, 16)
        g.vector.wait_ge(sem.lx, 16)
        g.vector.quantize_mx(T.tq[:, XB:TW], T.ts[:, XB:TW], T.xb[:]).then_inc(sem.qx, 1)
        g.vector.wait_ge(sem.lw, 16)
        g.vector.quantize_mx(T.wq[:], T.ws[:], T.wb[:]).then_inc(sem.qw, 1)

    if core in plan["tile"]:
        got = plan["tile"][core]
        lo = XB - got
        m = max(got, P)
        g.tensor.wait_ge(sem.qw if rank is not None else sem.hw, count["qw" if rank is not None else "hw"])
        if got < P:
            g.tensor.wait_ge(sem.qx if rank is not None else sem.hx, count["qx" if rank is not None else "hx"])
        if got:
            g.tensor.wait_ge(sem.tok, count["tok"])
        g.tensor.matmul_mx(T.ps[:, 0:m], T.wq[:], T.ws[:], T.tq[:, lo:lo + m], T.ts[:, lo:lo + m], True, False).then_inc(sem.mm, 1)
        g.tensor.wait_ge(sem.w2, count["w2"])
        g.tensor.matmul_mx(T.ps[:, 0:m], T.vq[:], T.vs[:], T.tq[:, lo:lo + m], T.ts[:, lo:lo + m], False, True).then_inc(sem.mm, 1)
        g.vector.wait_ge(sem.mm, 2)
        if got:
            g.vector.tensor_copy(T.rs[:, 0:got], T.ps[:, 0:got]).then_inc(sem.cp, 1)

    waited = set()
    for call in calls:
        for t in call:
            if t["need"] not in waited:
                waited.add(t["need"])
                g.wait_ge(sem[t["need"]], count[t["need"]])
        made = []
        for t in call:
            rid, pid = topo.addr(t["dst"], core)
            made.append((view(T, t["kind"], t["sb"], t["slo"], t["shi"]), view(T, t["kind"], t["db"], t["dlo"], t["dhi"]),
                         rid, pid, t["mask"], sem[t["sem"]]))
        if len(made) == 1:
            src, dst, rid, pid, mask, rsem = made[0]
            g.remote_dma(out_ap=dst, in_ap=src, remote_sem=rsem, local_sem=sem.loc, pid=pid, routing_id=rid,
                         dma_engine_mask=mask)
        else:
            g.remote_dma_fused([RemoteDMATransfer(dst_ids=[DstId(rid=rid, pnc=pid)], dma_engine_mask=mask, remote_sem=rsem,
                                                  src=src, dst=dst) for src, dst, rid, pid, mask, rsem in made],
                               local_sem=sem.loc)
    for name in ("hx", "hw"):
        if name in expect and name not in waited and not (core in plan["tile"] and (name == "hw" or plan["tile"][core] < P)):
            g.wait_ge(sem[name], count[name])
    if rank is not None:
        g.sync.wait_ge(sem.res, count["res"])
        g.sync.dma_start(T.y[:], T.yl[:]).then_inc(sem.st, 16)
        g.sync.wait_ge(sem.st, 16)
    if calls:
        g.wait_ge(sem.loc, count["loc"])
